import numpy as np
import ml_dtypes


def mxq(x, axis, fmt="e4m3"):
    dtype, down = {"e4m3": (ml_dtypes.float8_e4m3fn, 7), "e5m2": (ml_dtypes.float8_e5m2, 14)}[fmt]
    v = np.moveaxis(np.asarray(x, np.float32).astype(ml_dtypes.bfloat16).astype(np.float64), axis, -1)
    blocks = v.reshape(v.shape[:-1] + (-1, 32))
    amax = np.abs(blocks).max(-1, keepdims=True)
    byte = np.maximum(np.where(amax > 0, np.frexp(amax)[1] - 1 + 127, 0) - down, 1)
    scale = np.exp2(byte - 127.0)
    codes = (blocks / scale).astype(np.float32).astype(dtype).astype(np.float64)
    return np.moveaxis((codes * scale).reshape(v.shape), -1, axis)


WIDE = False


def mx_kscale(k):
    if not WIDE:
        return np.ones(k)
    levels = np.array([10, -10, 5, -5, 0])
    if k % 512:
        return np.exp2(np.random.permutation(np.resize(levels, k // 32))).repeat(32)
    a = np.empty((k // 512, 16))
    for p in range(k // 512):
        a[p, :8] = np.random.permutation(np.resize(levels, 8))
        for g in range(8):
            far = levels[np.abs(levels - a[p, g]) >= 10]
            a[p, g + 8] = far[np.random.randint(len(far))]
    return np.exp2(a.ravel()).repeat(32)


def f64(x):
    return np.asarray(x).astype(np.float64)


def striped(idx):
    return np.tile(idx.reshape(-1, 16).T, (8, 1)).astype(np.uint16)


def unstriped(offs):
    return offs[:16].T.reshape(-1).astype(np.int64)


def relu2(v):
    return np.maximum(v, 0.0) ** 2


K, T, S, N = 512, 4096, 1536, 128


def setup_inputs():
    n = np.random.standard_normal
    s = mx_kscale(K)[:, None]
    return {
        "xT": (n((K, T)) * s).astype(np.float32),
        "w": (n((K, N)) / np.sqrt(K) / s).astype(np.float32),
        "b": (0.3 * n((N, 1))).astype(np.float32),
        "offs": striped(np.random.permutation(T)[:S]),
    }


def reference(xT, w, b, offs):
    idx = unstriped(offs)
    xq = mxq(f64(xT)[:, idx], 0, "e4m3")
    y = mxq(f64(w), 0, "e4m3").T @ xq
    y = relu2(y + f64(b))
    return y

@@ -1,0 +1,124 @@
+from contextlib import ExitStack
+
+import concourse.mybir as mybir
+
+K, T, S, N = 512, 4096, 1536, 128
+P = 128
+PACK = 4
+SLICE = 512
+HALF = 256
+
+FLOPS = 2 * K * N * S
+
+F32 = mybir.dt.float32
+BF16 = mybir.dt.bfloat16
+U32 = mybir.dt.uint32
+U16 = mybir.dt.uint16
+U8 = mybir.dt.uint8
+FP8X4 = mybir.dt.float8_e4m3fn_x4
+RELU = mybir.ActivationFunctionType.Relu
+SQUARE = mybir.ActivationFunctionType.Square
+ADD = mybir.AluOpType.add
+MAX = mybir.AluOpType.max
+MULT = mybir.AluOpType.mult
+
+
+def tile_picked_pick_lin_relu2_sub_e_kernel(tc, xT, w, b, offs, out):
+    nc = tc.nc
+    with ExitStack() as ctx:
+        keep = ctx.enter_context(tc.tile_pool(name="keep", bufs=1))
+        psum = ctx.enter_context(tc.psum_pool(name="psum", bufs=1))
+
+        offsets = keep.tile([P, S // 16], U16, name="offsets")
+        planes = [keep.tile([P, T], F32, name=f"plane{t}") for t in range(PACK)]
+        w_raw = keep.tile([P, PACK, N], F32, name="w_raw")
+        bias = keep.tile([P, 1], F32, name="bias")
+        warm = keep.tile([P, 1], F32, name="warm")
+
+        x_rows = xT.rearrange("(p j) n -> p j n", j=PACK)
+        nc.sync.dma_start(planes[0][:], x_rows[:, 0, :])
+        nc.sync.dma_start(offsets[:], offs)
+        for t in range(1, PACK):
+            nc.sync.dma_start(planes[t][:], x_rows[:, t, :])
+        nc.sync.dma_start(w_raw[:], w.rearrange("(p j) m -> p j m", j=PACK))
+        nc.scalar.dma_start(bias[:], b)
+
+        nc.vector.memset(warm[:], 0.0)
+        nc.scalar.activation(warm[:], warm[:], RELU)
+
+        g01 = keep.tile([P, 2, S], F32, name="g01")
+        g2 = keep.tile([P, 2 * SLICE], F32, name="g2")
+        g3 = [keep.tile([P, SLICE], F32, name=f"g3_{s}") for s in range(2)]
+        grouped = [keep.tile([P, SLICE, PACK], BF16, name=f"grouped{s}", align_bytes=64) for s in range(3)]
+        codes = [keep.tile([P, SLICE], U32, name=f"codes{s}", align_bytes=64) for s in range(3)]
+        scales = [keep.tile([P, SLICE], U8, name=f"scales{s}", align_bytes=64) for s in range(3)]
+        w_grouped = keep.tile([P, N, PACK], BF16, name="w_grouped", align_bytes=64)
+        w_codes = keep.tile([P, N], U32, name="w_codes", align_bytes=64)
+        w_scales = keep.tile([P, N], U8, name="w_scales", align_bytes=64)
+
+        def list_part(s):
+            return offsets[:, s * SLICE // 16 : (s + 1) * SLICE // 16]
+
+        for t in range(2):
+            nc.vector.tensor_copy(g01[:, t, :], planes[t][:].indirect(offsets[:]))
+        for s in range(3):
+            cols = slice(s * SLICE, (s + 1) * SLICE)
+            nc.scalar.copy(grouped[s][:, :, 0:2], g01[:, :, cols].rearrange("p t n -> p n t"))
+        nc.vector.tensor_copy(g2[:], planes[2][:].indirect(offsets[:, 0 : 2 * SLICE // 16]))
+        nc.vector.tensor_copy(grouped[2][:, :, 2], planes[2][:].indirect(list_part(2)))
+        for s in range(2):
+            nc.scalar.copy(grouped[s][:, :, 2], g2[:, s * SLICE : (s + 1) * SLICE])
+
+        nc.scalar.copy(w_grouped[:], w_raw[:].rearrange("p j m -> p m j"))
+        for s in range(2):
+            nc.vector.tensor_copy(g3[s][:], planes[3][:].indirect(list_part(s)))
+            nc.scalar.copy(grouped[s][:, :, 3], g3[s][:])
+        nc.vector.quantize_mx(
+            out=w_codes[:].bitcast(FP8X4), scales=w_scales[:], in_=w_grouped[:].rearrange("p m j -> p (m j)")
+        )
+        nc.vector.tensor_copy(grouped[2][:, :, 3], planes[3][:].indirect(list_part(2)))
+
+        def quantise(s, a, z):
+            nc.vector.quantize_mx(
+                out=codes[s][:, a:z].bitcast(FP8X4),
+                scales=scales[s][:, a:z],
+                in_=grouped[s][:].rearrange("p n j -> p (n j)")[:, PACK * a : PACK * z],
+            )
+
+        def product(acc, s, a, z):
+            nc.tensor.matmul_mx(
+                out=acc[:],
+                lhsT=w_codes[:].bitcast(FP8X4),
+                lhsT_scale=w_scales[:],
+                rhs=codes[s][:, a:z].bitcast(FP8X4),
+                rhs_scale=scales[s][:, a:z],
+                start=True,
+                stop=True,
+            )
+
+        def finish(acc, col, width, on_scalar, queue):
+            kept = keep.tile([P, width], F32, name=f"kept{col}")
+            result = keep.tile([P, width], F32, name=f"result{col}")
+            if on_scalar:
+                nc.scalar.activation(kept[:], acc[:], RELU, bias=bias[:])
+                nc.scalar.activation(result[:], kept[:], SQUARE)
+            else:
+                nc.vector.tensor_scalar(kept[:], acc[:], bias[:], 0.0, ADD, MAX)
+                nc.vector.tensor_tensor(result[:], kept[:], kept[:], MULT)
+            queue.dma_start(out[:, col : col + width], result[:])
+
+        accs = [psum.tile([P, SLICE], F32, name=f"acc{s}") for s in range(2)]
+        halves = [psum.tile([P, HALF], F32, name=f"half{h}") for h in range(2)]
+
+        quantise(0, 0, SLICE)
+        product(accs[0], 0, 0, SLICE)
+        finish(accs[0], 0, SLICE, True, nc.sync)
+        quantise(1, 0, SLICE)
+        product(accs[1], 1, 0, SLICE)
+        quantise(2, 0, HALF)
+        product(halves[0], 2, 0, HALF)
+        quantise(2, HALF, SLICE)
+        product(halves[1], 2, HALF, SLICE)
+        finish(accs[1], SLICE, SLICE, False, nc.sync)
+        finish(halves[0], 2 * SLICE, HALF, True, nc.scalar)
+        finish(halves[1], 2 * SLICE + HALF, HALF, False, nc.sync)

@@ -46,37 +46,21 @@ def tile_picked_pick_lin_relu2_sub_e_kernel(tc, xT, w, b, offs, out):
         nc.vector.memset(warm[:], 0.0)
         nc.scalar.activation(warm[:], warm[:], RELU)
 
-        g01 = keep.tile([P, 2, S], F32, name="g01")
-        g2 = keep.tile([P, 2 * SLICE], F32, name="g2")
-        g3 = [keep.tile([P, SLICE], F32, name=f"g3_{s}") for s in range(2)]
+        g01 = [keep.tile([P, 2, SLICE], F32, name=f"g01_{s}") for s in range(2)]
+        g2 = keep.tile([P, SLICE], F32, name="g2")
+        g3 = keep.tile([P, SLICE], F32, name="g3")
         grouped = [keep.tile([P, SLICE, PACK], BF16, name=f"grouped{s}", align_bytes=64) for s in range(3)]
         codes = [keep.tile([P, SLICE], U32, name=f"codes{s}", align_bytes=64) for s in range(3)]
         scales = [keep.tile([P, SLICE], U8, name=f"scales{s}", align_bytes=64) for s in range(3)]
         w_grouped = keep.tile([P, N, PACK], BF16, name="w_grouped", align_bytes=64)
         w_codes = keep.tile([P, N], U32, name="w_codes", align_bytes=64)
         w_scales = keep.tile([P, N], U8, name="w_scales", align_bytes=64)
+        kept = keep.tile([P, S], F32, name="kept")
+        result = keep.tile([P, S], F32, name="result")
+        accs = [psum.tile([P, SLICE], F32, name=f"acc{i}") for i in range(6)]
 
         def list_part(s):
             return offsets[:, s * SLICE // 16 : (s + 1) * SLICE // 16]
-
-        for t in range(2):
-            nc.vector.tensor_copy(g01[:, t, :], planes[t][:].indirect(offsets[:]))
-        for s in range(3):
-            cols = slice(s * SLICE, (s + 1) * SLICE)
-            nc.scalar.copy(grouped[s][:, :, 0:2], g01[:, :, cols].rearrange("p t n -> p n t"))
-        nc.vector.tensor_copy(g2[:], planes[2][:].indirect(offsets[:, 0 : 2 * SLICE // 16]))
-        nc.vector.tensor_copy(grouped[2][:, :, 2], planes[2][:].indirect(list_part(2)))
-        for s in range(2):
-            nc.scalar.copy(grouped[s][:, :, 2], g2[:, s * SLICE : (s + 1) * SLICE])
-
-        nc.scalar.copy(w_grouped[:], w_raw[:].rearrange("p j m -> p m j"))
-        for s in range(2):
-            nc.vector.tensor_copy(g3[s][:], planes[3][:].indirect(list_part(s)))
-            nc.scalar.copy(grouped[s][:, :, 3], g3[s][:])
-        nc.vector.quantize_mx(
-            out=w_codes[:].bitcast(FP8X4), scales=w_scales[:], in_=w_grouped[:].rearrange("p m j -> p (m j)")
-        )
-        nc.vector.tensor_copy(grouped[2][:, :, 3], planes[3][:].indirect(list_part(2)))
 
         def quantise(s, a, z):
             nc.vector.quantize_mx(
@@ -85,9 +69,9 @@ def tile_picked_pick_lin_relu2_sub_e_kernel(tc, xT, w, b, offs, out):
                 in_=grouped[s][:].rearrange("p n j -> p (n j)")[:, PACK * a : PACK * z],
             )
 
-        def product(acc, s, a, z):
+        def product(i, s, a, z):
             nc.tensor.matmul_mx(
-                out=acc[:],
+                out=accs[i][:, 0 : z - a],
                 lhsT=w_codes[:].bitcast(FP8X4),
                 lhsT_scale=w_scales[:],
                 rhs=codes[s][:, a:z].bitcast(FP8X4),
@@ -96,29 +80,58 @@ def tile_picked_pick_lin_relu2_sub_e_kernel(tc, xT, w, b, offs, out):
                 stop=True,
             )
 
-        def finish(acc, col, width, on_scalar, queue):
-            kept = keep.tile([P, width], F32, name=f"kept{col}")
-            result = keep.tile([P, width], F32, name=f"result{col}")
-            if on_scalar:
-                nc.scalar.activation(kept[:], acc[:], RELU, bias=bias[:])
-                nc.scalar.activation(result[:], kept[:], SQUARE)
-            else:
-                nc.vector.tensor_scalar(kept[:], acc[:], bias[:], 0.0, ADD, MAX)
-                nc.vector.tensor_tensor(result[:], kept[:], kept[:], MULT)
-            queue.dma_start(out[:, col : col + width], result[:])
+        def relu_s(i, c, n):
+            nc.scalar.activation(kept[:, c : c + n], accs[i][:, 0:n], RELU, bias=bias[:])
 
-        accs = [psum.tile([P, SLICE], F32, name=f"acc{s}") for s in range(2)]
-        halves = [psum.tile([P, HALF], F32, name=f"half{h}") for h in range(2)]
+        def square_s(c, n):
+            nc.scalar.activation(result[:, c : c + n], kept[:, c : c + n], SQUARE)
 
-        quantise(0, 0, SLICE)
-        product(accs[0], 0, 0, SLICE)
-        finish(accs[0], 0, SLICE, True, nc.sync)
-        quantise(1, 0, SLICE)
-        product(accs[1], 1, 0, SLICE)
-        quantise(2, 0, HALF)
-        product(halves[0], 2, 0, HALF)
-        quantise(2, HALF, SLICE)
-        product(halves[1], 2, HALF, SLICE)
-        finish(accs[1], SLICE, SLICE, False, nc.sync)
-        finish(halves[0], 2 * SLICE, HALF, True, nc.scalar)
-        finish(halves[1], 2 * SLICE + HALF, HALF, False, nc.sync)
+        def relu_v(i, c, n):
+            nc.vector.tensor_scalar(kept[:, c : c + n], accs[i][:, 0:n], bias[:], 0.0, ADD, MAX)
+
+        def square_v(c, n):
+            nc.vector.tensor_tensor(result[:, c : c + n], kept[:, c : c + n], kept[:, c : c + n], MULT)
+
+        def store(queue, c, n):
+            queue.dma_start(out[:, c : c + n], result[:, c : c + n])
+
+        def gather(target, t, s):
+            nc.vector.tensor_copy(target, planes[t][:].indirect(list_part(s)))
+
+        for t in range(2):
+            for s in range(2):
+                gather(g01[s][:, t, :], t, s)
+            gather(grouped[2][:, :, t], t, 2)
+        for s in range(2):
+            nc.scalar.copy(grouped[s][:, :, 0:2], g01[s][:].rearrange("p t n -> p n t"))
+        gather(g2[:], 2, 0)
+        nc.scalar.copy(grouped[0][:, :, 2], g2[:])
+        for s in (1, 2):
+            gather(grouped[s][:, :, 2], 2, s)
+
+        nc.gpsimd.tensor_copy(w_grouped[:], w_raw[:].rearrange("p j m -> p m j"))
+        gather(grouped[2][:, :, 3], 3, 2)
+        gather(g3[:], 3, 0)
+        nc.scalar.copy(grouped[0][:, :, 3], g3[:])
+        nc.vector.quantize_mx(
+            out=w_codes[:].bitcast(FP8X4), scales=w_scales[:], in_=w_grouped[:].rearrange("p m j -> p (m j)")
+        )
+        quantise(2, 0, SLICE)
+        product(4, 2, 0, SLICE)
+        gather(grouped[1][:, :, 3], 3, 1)
+        relu_s(4, 2 * SLICE, SLICE)
+        square_s(2 * SLICE, SLICE)
+        store(nc.sync, 2 * SLICE, SLICE)
+        for s in range(2):
+            quantise(s, 0, SLICE)
+            for h in range(2):
+                product(2 * s + h, s, h * HALF, (h + 1) * HALF)
+        for s in range(2):
+            relu_s(2 * s, s * SLICE, HALF)
+            square_s(s * SLICE, HALF)
+            store(nc.sync, s * SLICE, HALF)
+        for s in range(2):
+            relu_v(2 * s + 1, s * SLICE + HALF, HALF)
+        for s in range(2):
+            square_v(s * SLICE + HALF, HALF)
+            store(nc.sync, s * SLICE + HALF, HALF)

from contextlib import ExitStack

import concourse.mybir as mybir

K, T, S, N = 512, 4096, 1536, 128
P = 128
PACK = 4
SLICE = 512
HALF = 256

FLOPS = 2 * K * N * S

F32 = mybir.dt.float32
BF16 = mybir.dt.bfloat16
U32 = mybir.dt.uint32
U16 = mybir.dt.uint16
U8 = mybir.dt.uint8
FP8X4 = mybir.dt.float8_e4m3fn_x4
RELU = mybir.ActivationFunctionType.Relu
SQUARE = mybir.ActivationFunctionType.Square
ADD = mybir.AluOpType.add
MAX = mybir.AluOpType.max
MULT = mybir.AluOpType.mult


def tile_picked_pick_lin_relu2_sub_e_kernel(tc, xT, w, b, offs, out):
    nc = tc.nc
    with ExitStack() as ctx:
        keep = ctx.enter_context(tc.tile_pool(name="keep", bufs=1))
        psum = ctx.enter_context(tc.psum_pool(name="psum", bufs=1))

        offsets = keep.tile([P, S // 16], U16, name="offsets")
        planes = [keep.tile([P, T], F32, name=f"plane{t}") for t in range(PACK)]
        w_raw = keep.tile([P, PACK, N], F32, name="w_raw")
        bias = keep.tile([P, 1], F32, name="bias")
        warm = keep.tile([P, 1], F32, name="warm")

        x_rows = xT.rearrange("(p j) n -> p j n", j=PACK)
        nc.sync.dma_start(planes[0][:], x_rows[:, 0, :])
        nc.sync.dma_start(offsets[:], offs)
        for t in range(1, PACK):
            nc.sync.dma_start(planes[t][:], x_rows[:, t, :])
        nc.sync.dma_start(w_raw[:], w.rearrange("(p j) m -> p j m", j=PACK))
        nc.scalar.dma_start(bias[:], b)

        nc.vector.memset(warm[:], 0.0)
        nc.scalar.activation(warm[:], warm[:], RELU)

        g01 = [keep.tile([P, 2, SLICE], F32, name=f"g01_{s}") for s in range(2)]
        g2 = keep.tile([P, SLICE], F32, name="g2")
        g3 = keep.tile([P, SLICE], F32, name="g3")
        grouped = [keep.tile([P, SLICE, PACK], BF16, name=f"grouped{s}", align_bytes=64) for s in range(3)]
        codes = [keep.tile([P, SLICE], U32, name=f"codes{s}", align_bytes=64) for s in range(3)]
        scales = [keep.tile([P, SLICE], U8, name=f"scales{s}", align_bytes=64) for s in range(3)]
        w_grouped = keep.tile([P, N, PACK], BF16, name="w_grouped", align_bytes=64)
        w_codes = keep.tile([P, N], U32, name="w_codes", align_bytes=64)
        w_scales = keep.tile([P, N], U8, name="w_scales", align_bytes=64)
        kept = keep.tile([P, S], F32, name="kept")
        result = keep.tile([P, S], F32, name="result")
        accs = [psum.tile([P, SLICE], F32, name=f"acc{i}") for i in range(6)]

        def list_part(s):
            return offsets[:, s * SLICE // 16 : (s + 1) * SLICE // 16]

        def quantise(s, a, z):
            nc.vector.quantize_mx(
                out=codes[s][:, a:z].bitcast(FP8X4),
                scales=scales[s][:, a:z],
                in_=grouped[s][:].rearrange("p n j -> p (n j)")[:, PACK * a : PACK * z],
            )

        def product(i, s, a, z):
            nc.tensor.matmul_mx(
                out=accs[i][:, 0 : z - a],
                lhsT=w_codes[:].bitcast(FP8X4),
                lhsT_scale=w_scales[:],
                rhs=codes[s][:, a:z].bitcast(FP8X4),
                rhs_scale=scales[s][:, a:z],
                start=True,
                stop=True,
            )

        def relu_s(i, c, n):
            nc.scalar.activation(kept[:, c : c + n], accs[i][:, 0:n], RELU, bias=bias[:])

        def square_s(c, n):
            nc.scalar.activation(result[:, c : c + n], kept[:, c : c + n], SQUARE)

        def relu_v(i, c, n):
            nc.vector.tensor_scalar(kept[:, c : c + n], accs[i][:, 0:n], bias[:], 0.0, ADD, MAX)

        def square_v(c, n):
            nc.vector.tensor_tensor(result[:, c : c + n], kept[:, c : c + n], kept[:, c : c + n], MULT)

        def store(queue, c, n):
            queue.dma_start(out[:, c : c + n], result[:, c : c + n])

        def gather(target, t, s):
            nc.vector.tensor_copy(target, planes[t][:].indirect(list_part(s)))

        for t in range(2):
            for s in range(2):
                gather(g01[s][:, t, :], t, s)
            gather(grouped[2][:, :, t], t, 2)
        for s in range(2):
            nc.scalar.copy(grouped[s][:, :, 0:2], g01[s][:].rearrange("p t n -> p n t"))
        gather(g2[:], 2, 0)
        nc.scalar.copy(grouped[0][:, :, 2], g2[:])
        for s in (1, 2):
            gather(grouped[s][:, :, 2], 2, s)

        nc.gpsimd.tensor_copy(w_grouped[:], w_raw[:].rearrange("p j m -> p m j"))
        gather(grouped[2][:, :, 3], 3, 2)
        gather(g3[:], 3, 0)
        nc.scalar.copy(grouped[0][:, :, 3], g3[:])
        nc.vector.quantize_mx(
            out=w_codes[:].bitcast(FP8X4), scales=w_scales[:], in_=w_grouped[:].rearrange("p m j -> p (m j)")
        )
        quantise(2, 0, SLICE)
        product(4, 2, 0, SLICE)
        gather(grouped[1][:, :, 3], 3, 1)
        relu_s(4, 2 * SLICE, SLICE)
        square_s(2 * SLICE, SLICE)
        store(nc.sync, 2 * SLICE, SLICE)
        for s in range(2):
            quantise(s, 0, SLICE)
            for h in range(2):
                product(2 * s + h, s, h * HALF, (h + 1) * HALF)
        for s in range(2):
            relu_s(2 * s, s * SLICE, HALF)
            square_s(s * SLICE, HALF)
            store(nc.sync, s * SLICE, HALF)
        for s in range(2):
            relu_v(2 * s + 1, s * SLICE + HALF, HALF)
        for s in range(2):
            square_v(s * SLICE + HALF, HALF)
            store(nc.sync, s * SLICE + HALF, HALF)
